import numpy as np, ml_dtypes
CORES = [2,10,50,58,66,74,122]
N = 7
TK = 256
WID = [128,96,256,224,32,224,32]
def setup_inputs(rng):
    return {"x": rng.standard_normal((N, 128, TK), dtype=np.float32).astype(ml_dtypes.bfloat16), "w": rng.standard_normal((N, 128, 128), dtype=np.float32).astype(ml_dtypes.bfloat16)}
def setup_inputs_big(rng):
    d = setup_inputs(rng)
    for k in ("x", "w"): d[k] = (d[k].astype(np.float32) * 1024.0).astype(d[k].dtype)
    return d
def setup_inputs_small(rng):
    d = setup_inputs(rng)
    for k in ("x", "w"): d[k] = (d[k].astype(np.float32) * (1 / 1024.0)).astype(d[k].dtype)
    return d
def setup_inputs_apart(rng):
    d = setup_inputs(rng)
    f = (10.0 ** rng.permutation(np.linspace(-1.5, 1.5, N))).astype(np.float32).reshape(N, 1, 1)
    for k in ("x", "w"): d[k] = (d[k].astype(np.float32) * f).astype(d[k].dtype)
    return d
def setup_inputs_neg(rng):
    d = setup_inputs(rng)
    d["x"] = (np.abs(d["x"].astype(np.float32)) * 1048576.0).astype(d["x"].dtype); d["w"] = (-np.abs(d["w"].astype(np.float32))).astype(d["w"].dtype)
    return d
def whole(x, w):
    X, W = x.astype(np.float64), w.astype(np.float64)
    y = np.stack([np.max([W[j].T @ X[r] for j in range(N)], axis=0) for r in range(N)])
    return {"y": y.astype(ml_dtypes.bfloat16)}
def reference(x, w):
    o = whole(x, w)["y"].copy()
    for r in range(N):
        o[r][:, WID[r]:] = np.nan
    return {"y": o}

from concourse.bass import DstId, RemoteDMATransfer
from concourse.mybir import AluOpType

N = 7
D = 128
TK = 256
BANK = 512

SCRATCH = {
    "wall": ("sbuf", [128, N * D], "bfloat16"),
    "xs": ("sbuf", [128, TK], "bfloat16"),
    "acc": ("sbuf", [128, TK], "float32"),
    "ys": ("sbuf", [128, TK], "bfloat16"),
}
for _j in range(N):
    SCRATCH["ps%d" % _j] = ("psum", [128, BANK], "float32")

SEMAPHORES = (["wld", "xld", "sent", "stored"] + ["arr%d" % j for j in range(N)]
              + ["mm%d" % j for j in range(N)] + ["vv%d" % j for j in range(N)])


def _bits(mask):
    return bin(mask).count("1")


def rank_program(g, core, T, topo):
    r = T.rank_of(core)
    if r is None:
        return
    S = T.sem
    wid = T.tables["WID"][r]
    n = len(T.cores)

    def slot(j):
        return T.wall[:, j * D:(j + 1) * D]

    g.sync.dma_start(slot(r), T.w[:, :]).then_inc(S.wld, 16)
    g.scalar.dma_start(T.xs[:, :wid], T.x[:, :wid]).then_inc(S.xld, 16)

    out_order = [(r + s) % n for s in range(1, n)]
    mask = None
    ids = []
    for d in out_order:
        dst = T.cores[d]
        assert topo.may_write(core, dst)
        m = topo.mask(core, dst)
        mask = m if mask is None else (mask & m)
        rid, pid, _ = topo.addr(dst)
        ids.append(DstId(rid=rid, pnc=pid))
    g.wait_ge(S.wld, 16)
    g.remote_dma_fused(
        [RemoteDMATransfer(dst_ids=ids, dma_engine_mask=mask, remote_sem=S["arr%d" % r],
                           srcs=[slot(r)], dsts=[slot(r) for _ in out_order], alu_op=0)],
        local_sem=S.sent)

    in_order = [r] + [(r - s) % n for s in range(1, n)]
    g.tensor.wait_ge(S.wld, 16)
    g.tensor.wait_ge(S.xld, 16)
    for j in in_order:
        if j != r:
            src = T.cores[j]
            m = None
            for d in range(n):
                if d != j:
                    mm = topo.mask(src, T.cores[d])
                    m = mm if m is None else (m & mm)
            g.tensor.wait_ge(S["arr%d" % j], _bits(m))
        g.tensor.matmul(T["ps%d" % j][:, :wid], slot(j), T.xs[:, :wid], True, True).then_inc(S["mm%d" % j], 1)

    for k, j in enumerate(in_order):
        g.vector.wait_ge(S["mm%d" % j], 1)
        p = T["ps%d" % j][:, :wid]
        if k == 0:
            g.vector.tensor_copy(T.acc[:, :wid], p).then_inc(S.vv0, 1)
            continue
        g.vector.wait_ge(S["vv%d" % (k - 1)], 1)
        out = T.ys[:, :wid] if k == n - 1 else T.acc[:, :wid]
        g.vector.tensor_tensor(out, T.acc[:, :wid], p, AluOpType.max).then_inc(S["vv%d" % k], 1)

    g.sync.wait_ge(S["vv%d" % (n - 1)], 1)
    g.sync.dma_start(T.y[:, :wid], T.ys[:, :wid]).then_inc(S.stored, 16)
    g.sync.wait_ge(S.stored, 16)
    g.wait_ge(S.sent, _bits(mask))
